import numpy as np
import ml_dtypes


def mxq(x, axis, fmt="e4m3"):
    dtype, down = {"e4m3": (ml_dtypes.float8_e4m3fn, 7), "e5m2": (ml_dtypes.float8_e5m2, 14)}[fmt]
    v = np.moveaxis(np.asarray(x, np.float32).astype(ml_dtypes.bfloat16).astype(np.float64), axis, -1)
    blocks = v.reshape(v.shape[:-1] + (-1, 32))
    amax = np.abs(blocks).max(-1, keepdims=True)
    byte = np.maximum(np.where(amax > 0, np.frexp(amax)[1] - 1 + 127, 0) - down, 1)
    scale = np.exp2(byte - 127.0)
    codes = (blocks / scale).astype(np.float32).astype(dtype).astype(np.float64)
    return np.moveaxis((codes * scale).reshape(v.shape), -1, axis)


WIDE = False


def mx_kscale(k):
    if not WIDE:
        return np.ones(k)
    levels = np.array([10, -10, 5, -5, 0])
    if k % 512:
        return np.exp2(np.random.permutation(np.resize(levels, k // 32))).repeat(32)
    a = np.empty((k // 512, 16))
    for p in range(k // 512):
        a[p, :8] = np.random.permutation(np.resize(levels, 8))
        for g in range(8):
            far = levels[np.abs(levels - a[p, g]) >= 10]
            a[p, g + 8] = far[np.random.randint(len(far))]
    return np.exp2(a.ravel()).repeat(32)


def f64(x):
    return np.asarray(x).astype(np.float64)


def striped(idx):
    return np.tile(np.asarray(idx).reshape(-1, 16).T, (8, 1)).astype(np.uint16)


def unstriped(offs):
    return offs[:16].T.reshape(-1).astype(np.int64)


E2M1 = np.array([0.0, 0.5, 1.0, 1.5, 2.0, 3.0, 4.0, 6.0, -0.0, -0.5, -1.0, -1.5, -2.0, -3.0, -4.0, -6.0])


def pack_weight(w, fmt):
    k, n = w.shape
    w = f64(np.asarray(w, np.float32).astype(ml_dtypes.bfloat16)).reshape(k // 32, 32, n)
    amax = np.abs(w).max(1)
    if fmt == "e4m3":
        byte = np.frexp(amax)[1] - 1 + 127 - 7
    else:
        mant, ex = np.frexp(amax / 6.0)
        byte = np.where(mant > 0.5, ex, ex - 1) + 127
    byte = np.clip(np.where(amax > 0, byte, 1), 1, 254)
    scaled = (w * np.exp2(127.0 - byte)[:, None, :]).reshape(k, n).astype(np.float32)
    by_word = np.ascontiguousarray(scaled.reshape(k // 512, 128, 4, n).transpose(0, 1, 3, 2))
    if fmt == "e4m3":
        words = by_word.astype(ml_dtypes.float8_e4m3fn).view(np.uint8)
    else:
        c = by_word.astype(ml_dtypes.float4_e2m1fn).view(np.uint8) & 0xF
        words = (c[..., 0::2] | (c[..., 1::2] << 4)).reshape(k // 512, 128, 2 * n)
    return np.ascontiguousarray(words), np.ascontiguousarray(byte.astype(np.uint8).reshape(k // 512, 16, n))


def unpack_weight(words, scales, fmt):
    g, _, n = scales.shape
    words = np.ascontiguousarray(words).reshape(g, 128, n, -1)
    if fmt == "e4m3":
        vals = words.view(ml_dtypes.float8_e4m3fn).astype(np.float64)
    else:
        nib = np.empty((g, 128, n, 4), np.uint8)
        nib[..., 0::2] = words & 0xF
        nib[..., 1::2] = words >> 4
        vals = E2M1[nib]
    vals = vals * np.repeat(np.exp2(scales.astype(np.float64) - 127.0), 8, axis=1)[..., None]
    return vals.transpose(0, 1, 3, 2).reshape(g * 512, n)


def e4m3fn_bytes(y):
    return np.clip(np.asarray(y, np.float64), -448.0, 448.0).astype(np.float32).astype(ml_dtypes.float8_e4m3fn).view(np.uint8)


def e4m3fn_values(b):
    return np.asarray(b, np.uint8).view(ml_dtypes.float8_e4m3fn).astype(np.float64)


K, T, J, R, F, Z, C, V, I, N = 512, 1024, 256, 512, 512, 1024, 512, 1024, 256, 256


def setup_inputs():
    n = np.random.standard_normal
    idx = np.random.permutation(T)[:J]
    idx2 = np.random.permutation(Z)[:J]
    idx3 = np.random.permutation(V)[:I]
    idx4 = np.random.permutation(C)[:I]
    idx5 = np.random.permutation(C)[:J]
    fk = mx_kscale(K)
    ff = mx_kscale(F)
    fr = mx_kscale(R)
    xtp = pack_weight(n((K, T)) / fk[:, None], "e2m1")
    xop = pack_weight(n((F, Z)) / ff[:, None], "e4m3")
    wp = pack_weight(n((K, R)) * 1 / np.sqrt(K) * fk[:, None] * fr, "e4m3")
    w0p = pack_weight(n((F, R)) * 1 / np.sqrt(F) * ff[:, None] * fr, "e2m1")
    wbp = pack_weight(n((R, N)) * 1 / np.sqrt(R) / fr[:, None], "e2m1")
    return {
        "xt_words": xtp[0],
        "xt_scales": xtp[1],
        "xo_words": xop[0],
        "xo_scales": xop[1],
        "w_words": wp[0],
        "w_scales": wp[1],
        "w0_words": w0p[0],
        "w0_scales": w0p[1],
        "ca": e4m3fn_bytes(60.0 * n((R, V))),
        "st": (np.random.uniform(0.008, 0.024, (R, 1)) * fr[:, None]).astype(np.float32),
        "wb_words": wbp[0],
        "wb_scales": wbp[1],
        "offs": striped(idx),
        "offs2": striped(idx2),
        "offs3": striped(idx3),
        "offs4": striped(idx4),
        "offs5": striped(idx5),
    }


def reference(xt_words, xt_scales, xo_words, xo_scales, w_words, w_scales, w0_words, w0_scales, ca, st, wb_words, wb_scales, offs, offs2, offs3, offs4, offs5):
    idx = unstriped(offs)
    idx2 = unstriped(offs2)
    idx3 = unstriped(offs3)
    idx4 = unstriped(offs4)
    idx5 = unstriped(offs5)
    xtu = unpack_weight(xt_words, xt_scales, "e2m1")
    xou = unpack_weight(xo_words, xo_scales, "e4m3")
    wu = unpack_weight(w_words, w_scales, "e4m3")
    w0u = unpack_weight(w0_words, w0_scales, "e2m1")
    wbu = unpack_weight(wb_words, wb_scales, "e2m1")
    xtidxg = xtu[:, idx]
    xoidx2g = xou[:, idx2]
    a = wu.T @ xtidxg + w0u.T @ xoidx2g
    g1 = e4m3fn_values(ca)[:, idx3] * f64(st)
    pw = np.zeros((R, C))
    pw[:, idx4] = g1
    hid = np.maximum(a - pw[:, idx5], 0.0)
    hidq = mxq(hid, 0, "e4m3")
    p = wbu.T @ hidq
    return p

@@ -1,0 +1,155 @@
+from contextlib import ExitStack
+
+import concourse.mybir as mybir
+
+K, T, J, R, F, Z, C, V, I, N = 512, 1024, 256, 512, 512, 1024, 512, 1024, 256, 256
+FLOPS = 2 * J * (K * R + F * R + R * N)
+
+F32 = mybir.dt.float32
+BF16 = mybir.dt.bfloat16
+I32 = mybir.dt.int32
+U32 = mybir.dt.uint32
+U16 = mybir.dt.uint16
+U8 = mybir.dt.uint8
+FP8 = mybir.dt.float8_e4m3fn
+FP8X4 = mybir.dt.float8_e4m3fn_x4
+FP4X4 = mybir.dt.float4_e2m1fn_x4
+ALU = mybir.AluOpType
+ACT = mybir.ActivationFunctionType
+
+P = 128
+PACK = 4
+QUADS = 4
+
+
+def tile_list_postedcodes_kernel(tc, xt_words, xt_scales, xo_words, xo_scales, w_words, w_scales, w0_words, w0_scales,
+                                      ca, st, wb_words, wb_scales, offs, offs2, offs3, offs4, offs5, out):
+    nc = tc.nc
+    with ExitStack() as ctx:
+        lists = ctx.enter_context(tc.tile_pool(name="lists", bufs=1))
+        sb = ctx.enter_context(tc.tile_pool(name="sb", bufs=1))
+        ps = ctx.enter_context(tc.psum_pool(name="ps", bufs=1))
+
+        def tile(name, cols, dtype):
+            return sb.tile([P, cols], dtype, name=name, align_bytes=64)
+
+        def load_list(name, src):
+            held = lists.tile([P, src.shape[1]], U16, name=name)
+            nc.sync.dma_start(held[:], src)
+            return held
+
+        def load_words(queue, name, src, cols, dtype):
+            held = tile(name, cols, dtype)
+            queue.dma_start(held[:].bitcast(I32), src.bitcast(I32))
+            return held
+
+        def zeroed_plane(name, cols):
+            plane = tile(name, cols, U8)
+            nc.vector.memset(plane[:].bitcast(I32), 0)
+            return plane
+
+        def load_plane(queue, plane, src):
+            for q in range(QUADS):
+                queue.dma_start(plane[32 * q : 32 * q + 4, :].bitcast(I32), src[0, 4 * q : 4 * q + 4, :].bitcast(I32))
+
+        def deal(engine_copy, name, src, dtype):
+            dealt = tile(name, R, dtype)
+            engine_copy(dealt[:].rearrange("p (t m) -> p m t", t=PACK), src[:].rearrange("p (m t) -> p m t", t=PACK))
+            return dealt
+
+        xt_plane = zeroed_plane("xt_plane", T)
+        w_plane = zeroed_plane("w_plane", R)
+        boards = [tile("board%d" % t, C, F32) for t in range(PACK)]
+        for t in range(PACK):
+            (nc.vector if t < 2 else nc.gpsimd).memset(boards[t][:], 0.0)
+        xo_plane = zeroed_plane("xo_plane", Z)
+        w0_plane = zeroed_plane("w0_plane", R)
+        wb_plane = zeroed_plane("wb_plane", N)
+
+        ca_rows = ca.rearrange("(p t) v -> p t v", t=PACK)
+        stores = [tile("store%d" % t, V, U8) for t in range(PACK)]
+        l3 = load_list("l3", offs3)
+        nc.sync.dma_start(stores[0][:], ca_rows[:, 0, :])
+        w_sb = load_words(nc.sync, "w_sb", w_words[0].rearrange("p n t -> p (n t)"), R, U32)
+        l4 = load_list("l4", offs4)
+        for t in range(1, PACK):
+            nc.sync.dma_start(stores[t][:], ca_rows[:, t, :])
+        steps = tile("steps", PACK, F32)
+        nc.sync.dma_start(steps[:], st.rearrange("(p t) o -> p (t o)", t=PACK))
+        l1 = load_list("l1", offs)
+        xt_sb = load_words(nc.sync, "xt_sb", xt_words[0], T, U16)
+        load_plane(nc.sync, xt_plane, xt_scales)
+        load_plane(nc.sync, w_plane, w_scales)
+        l2 = load_list("l2", offs2)
+        xo_sb = load_words(nc.sync, "xo_sb", xo_words[0].rearrange("p n t -> p (n t)"), Z, U32)
+        load_plane(nc.sync, xo_plane, xo_scales)
+        w0_sb = load_words(nc.sync, "w0_sb", w0_words[0], R, U16)
+        load_plane(nc.sync, w0_plane, w0_scales)
+        l5 = load_list("l5", offs5)
+        wb_sb = load_words(nc.sync, "wb_sb", wb_words[0], N, U16)
+        load_plane(nc.sync, wb_plane, wb_scales)
+
+        picked = [tile("picked%d" % t, I, U8) for t in range(PACK)]
+        bars = [tile("bars%d" % t, I, F32) for t in range(PACK)]
+        taken = [tile("taken%d" % t, J, F32) for t in range(PACK)]
+        for t in range(PACK):
+            nc.vector.tensor_copy(picked[t][:], stores[t][:].indirect(l3[:]))
+        w_d = deal(nc.scalar.copy, "w_d", w_sb, U32)
+        nc.scalar.activation(bars[0][:], picked[0][:].bitcast(FP8), ACT.Copy)
+        nc.scalar.activation(boards[0][:].indirect(l4[:]), bars[0][:], ACT.Copy, scale=steps[:, 0:1])
+        for t in (1, 3, 2):
+            nc.vector.tensor_scalar(bars[t][:], picked[t][:].bitcast(FP8), steps[:, t : t + 1], None, ALU.mult)
+        for t in (1, 2):
+            nc.scalar.activation(boards[t][:].indirect(l4[:]), bars[t][:], ACT.Copy)
+        nc.vector.tensor_copy(boards[3][:].indirect(l4[:]), bars[3][:])
+
+        xt_g = tile("xt_g", J, U16)
+        xt_gs = tile("xt_gs", J, U8)
+        xo_g = tile("xo_g", J, U32)
+        xo_gs = tile("xo_gs", J, U8)
+        nc.vector.tensor_copy(xt_g[:], xt_sb[:].indirect(l1[:]))
+        nc.vector.tensor_copy(xt_gs[:], xt_plane[:].indirect(l1[:]))
+        w_ds = deal(nc.vector.tensor_copy, "w_ds", w_plane, U8)
+        nc.vector.tensor_copy(xo_g[:], xo_sb[:].indirect(l2[:]))
+        nc.vector.tensor_copy(xo_gs[:], xo_plane[:].indirect(l2[:]))
+        w0_d = deal(nc.scalar.copy, "w0_d", w0_sb, U16)
+        w0_ds = deal(nc.vector.tensor_copy, "w0_ds", w0_plane, U8)
+
+        for t in range(PACK - 1):
+            nc.scalar.activation(taken[t][:], boards[t][:].indirect(l5[:]), ACT.Copy)
+        nc.vector.tensor_copy(taken[PACK - 1][:], boards[PACK - 1][:].indirect(l5[:]))
+
+        accs = [ps.tile([P, J], F32, name="acc%d" % t) for t in range(PACK)]
+        for t in range(PACK):
+            cols = slice(t * P, (t + 1) * P)
+            nc.tensor.matmul_mx(accs[t][:], lhsT=w_d[:, cols].bitcast(FP8X4), lhsT_scale=w_ds[:, cols],
+                                rhs=xt_g[:].bitcast(FP4X4), rhs_scale=xt_gs[:], start=True, stop=False)
+        diff = sb.tile([P, PACK, J], F32, name="diff")
+        for t in range(PACK):
+            cols = slice(t * P, (t + 1) * P)
+            nc.tensor.matmul_mx(accs[t][:], lhsT=w0_d[:, cols].bitcast(FP4X4), lhsT_scale=w0_ds[:, cols],
+                                rhs=xo_g[:].bitcast(FP8X4), rhs_scale=xo_gs[:], start=False, stop=True)
+        halves = [slice(h * P, (h + 1) * P) for h in range(J // P)]
+        for t in range(PACK - 1):
+            nc.vector.tensor_tensor(diff[:, t, :], accs[t][:], taken[t][:], ALU.subtract)
+        t = PACK - 1
+        for half in halves:
+            nc.vector.tensor_tensor(diff[:, t, half], accs[t][:, half], taken[t][:, half], ALU.subtract)
+
+        hids = [sb.tile([P, P, PACK], BF16, name="hid%d" % h, align_bytes=64) for h in range(2)]
+        hid_codes = [tile("hid_codes%d" % h, P, U32) for h in range(2)]
+        hid_scales = [tile("hid_scales%d" % h, P, U8) for h in range(2)]
+        for h, half in enumerate(halves):
+            nc.vector.tensor_scalar(hids[h][:], diff[:, :, half].rearrange("p t j -> p j t"), 0.0, None, ALU.max)
+        for h in range(2):
+            nc.vector.quantize_mx(hid_codes[h][:].bitcast(FP8X4), hid_scales[h][:], hids[h][:].rearrange("p j t -> p (j t)"))
+
+        for h, half in enumerate(halves):
+            for u, (copy, queue) in enumerate(((nc.scalar.copy, nc.scalar), (nc.vector.tensor_copy, nc.sync))):
+                cols = slice(u * P, (u + 1) * P)
+                res = ps.tile([P, P], F32, name="res%d%d" % (h, u))
+                nc.tensor.matmul_mx(res[:], lhsT=wb_sb[:, cols].bitcast(FP4X4), lhsT_scale=wb_plane[:, cols],
+                                    rhs=hid_codes[h][:].bitcast(FP8X4), rhs_scale=hid_scales[h][:], start=True, stop=True)
+                done = tile("done%d%d" % (h, u), P, F32)
+                copy(done[:], res[:])
+                queue.dma_start(out[cols, half], done[:])

@@ -54,7 +54,8 @@ def tile_list_postedcodes_kernel(tc, xt_words, xt_scales, xo_words, xo_scales, w
 
         def deal(engine_copy, name, src, dtype):
             dealt = tile(name, R, dtype)
-            engine_copy(dealt[:].rearrange("p (t m) -> p m t", t=PACK), src[:].rearrange("p (m t) -> p m t", t=PACK))
+            walk = "p m t" if dtype == U32 else "p t m"
+            engine_copy(dealt[:].rearrange("p (t m) -> " + walk, t=PACK), src[:].rearrange("p (m t) -> " + walk, t=PACK))
             return dealt
 
         xt_plane = zeroed_plane("xt_plane", T)
@@ -70,15 +71,16 @@ def tile_list_postedcodes_kernel(tc, xt_words, xt_scales, xo_words, xo_scales, w
         stores = [tile("store%d" % t, V, U8) for t in range(PACK)]
         l3 = load_list("l3", offs3)
         nc.sync.dma_start(stores[0][:], ca_rows[:, 0, :])
-        w_sb = load_words(nc.sync, "w_sb", w_words[0].rearrange("p n t -> p (n t)"), R, U32)
+        nc.sync.dma_start(stores[1][:], ca_rows[:, 1, :])
         l4 = load_list("l4", offs4)
-        for t in range(1, PACK):
+        for t in range(2, PACK):
             nc.sync.dma_start(stores[t][:], ca_rows[:, t, :])
         steps = tile("steps", PACK, F32)
         nc.sync.dma_start(steps[:], st.rearrange("(p t) o -> p (t o)", t=PACK))
         l1 = load_list("l1", offs)
         xt_sb = load_words(nc.sync, "xt_sb", xt_words[0], T, U16)
         load_plane(nc.sync, xt_plane, xt_scales)
+        w_sb = load_words(nc.sync, "w_sb", w_words[0].rearrange("p n t -> p (n t)"), R, U32)
         load_plane(nc.sync, w_plane, w_scales)
         l2 = load_list("l2", offs2)
         xo_sb = load_words(nc.sync, "xo_sb", xo_words[0].rearrange("p n t -> p (n t)"), Z, U32)
@@ -94,7 +96,6 @@ def tile_list_postedcodes_kernel(tc, xt_words, xt_scales, xo_words, xo_scales, w
         taken = [tile("taken%d" % t, J, F32) for t in range(PACK)]
         for t in range(PACK):
             nc.vector.tensor_copy(picked[t][:], stores[t][:].indirect(l3[:]))
-        w_d = deal(nc.scalar.copy, "w_d", w_sb, U32)
         nc.scalar.activation(bars[0][:], picked[0][:].bitcast(FP8), ACT.Copy)
         nc.scalar.activation(boards[0][:].indirect(l4[:]), bars[0][:], ACT.Copy, scale=steps[:, 0:1])
         for t in (1, 3, 2):
@@ -103,6 +104,7 @@ def tile_list_postedcodes_kernel(tc, xt_words, xt_scales, xo_words, xo_scales, w
             nc.scalar.activation(boards[t][:].indirect(l4[:]), bars[t][:], ACT.Copy)
         nc.vector.tensor_copy(boards[3][:].indirect(l4[:]), bars[3][:])
 
+        w_d = deal(nc.scalar.copy, "w_d", w_sb, U32)
         xt_g = tile("xt_g", J, U16)
         xt_gs = tile("xt_gs", J, U8)
         xo_g = tile("xo_g", J, U32)
@@ -140,7 +142,8 @@ def tile_list_postedcodes_kernel(tc, xt_words, xt_scales, xo_words, xo_scales, w
         hid_codes = [tile("hid_codes%d" % h, P, U32) for h in range(2)]
         hid_scales = [tile("hid_scales%d" % h, P, U8) for h in range(2)]
         for h, half in enumerate(halves):
-            nc.vector.tensor_scalar(hids[h][:], diff[:, :, half].rearrange("p t j -> p j t"), 0.0, None, ALU.max)
+            nc.vector.tensor_scalar(hids[h][:].rearrange("p (c i) t -> p c t i", i=4),
+                                    diff[:, :, half].rearrange("p t (c i) -> p c t i", i=4), 0.0, None, ALU.max)
         for h in range(2):
             nc.vector.quantize_mx(hid_codes[h][:].bitcast(FP8X4), hid_scales[h][:], hids[h][:].rearrange("p j t -> p (j t)"))
 

@@ -30,8 +30,8 @@ def tile_list_postedcodes_kernel(tc, xt_words, xt_scales, xo_words, xo_scales, w
         sb = ctx.enter_context(tc.tile_pool(name="sb", bufs=1))
         ps = ctx.enter_context(tc.psum_pool(name="ps", bufs=1))
 
-        def tile(name, cols, dtype):
-            return sb.tile([P, cols], dtype, name=name, align_bytes=64)
+        def tile(name, cols, dtype, tag=None):
+            return sb.tile([P, cols], dtype, name=name, tag=tag or name, align_bytes=64)
 
         def load_list(name, src):
             held = lists.tile([P, src.shape[1]], U16, name=name)
@@ -43,28 +43,28 @@ def tile_list_postedcodes_kernel(tc, xt_words, xt_scales, xo_words, xo_scales, w
             queue.dma_start(held[:].bitcast(I32), src.bitcast(I32))
             return held
 
-        def zeroed_plane(name, cols):
+        def zeroed_plane(name, cols, engine=nc.vector):
             plane = tile(name, cols, U8)
-            nc.vector.memset(plane[:].bitcast(I32), 0)
+            engine.memset(plane[:].bitcast(I32), 0)
             return plane
 
         def load_plane(queue, plane, src):
             for q in range(QUADS):
                 queue.dma_start(plane[32 * q : 32 * q + 4, :].bitcast(I32), src[0, 4 * q : 4 * q + 4, :].bitcast(I32))
 
-        def deal(engine_copy, name, src, dtype):
-            dealt = tile(name, R, dtype)
+        def deal(engine_copy, name, src, dtype, tag=None):
+            dealt = tile(name, R, dtype, tag)
             walk = "p m t" if dtype == U32 else "p t m"
             engine_copy(dealt[:].rearrange("p (t m) -> " + walk, t=PACK), src[:].rearrange("p (m t) -> " + walk, t=PACK))
             return dealt
 
+        w0_plane = zeroed_plane("w0_plane", R, nc.gpsimd)
         xt_plane = zeroed_plane("xt_plane", T)
         w_plane = zeroed_plane("w_plane", R)
         boards = [tile("board%d" % t, C, F32) for t in range(PACK)]
         for t in range(PACK):
-            (nc.vector if t < 2 else nc.gpsimd).memset(boards[t][:], 0.0)
+            nc.vector.memset(boards[t][:], 0.0)
         xo_plane = zeroed_plane("xo_plane", Z)
-        w0_plane = zeroed_plane("w0_plane", R)
         wb_plane = zeroed_plane("wb_plane", N)
 
         ca_rows = ca.rearrange("(p t) v -> p t v", t=PACK)
@@ -72,21 +72,21 @@ def tile_list_postedcodes_kernel(tc, xt_words, xt_scales, xo_words, xo_scales, w
         l3 = load_list("l3", offs3)
         nc.sync.dma_start(stores[0][:], ca_rows[:, 0, :])
         nc.sync.dma_start(stores[1][:], ca_rows[:, 1, :])
+        w_sb = load_words(nc.sync, "w_sb", w_words[0].rearrange("p n t -> p (n t)"), R, U32)
         l4 = load_list("l4", offs4)
         for t in range(2, PACK):
             nc.sync.dma_start(stores[t][:], ca_rows[:, t, :])
         steps = tile("steps", PACK, F32)
         nc.sync.dma_start(steps[:], st.rearrange("(p t) o -> p (t o)", t=PACK))
+        load_plane(nc.gpsimd, w0_plane, w0_scales)
         l1 = load_list("l1", offs)
         xt_sb = load_words(nc.sync, "xt_sb", xt_words[0], T, U16)
         load_plane(nc.sync, xt_plane, xt_scales)
-        w_sb = load_words(nc.sync, "w_sb", w_words[0].rearrange("p n t -> p (n t)"), R, U32)
         load_plane(nc.sync, w_plane, w_scales)
+        w0_sb = load_words(nc.sync, "w0_sb", w0_words[0], R, U16)
         l2 = load_list("l2", offs2)
         xo_sb = load_words(nc.sync, "xo_sb", xo_words[0].rearrange("p n t -> p (n t)"), Z, U32)
         load_plane(nc.sync, xo_plane, xo_scales)
-        w0_sb = load_words(nc.sync, "w0_sb", w0_words[0], R, U16)
-        load_plane(nc.sync, w0_plane, w0_scales)
         l5 = load_list("l5", offs5)
         wb_sb = load_words(nc.sync, "wb_sb", wb_words[0], N, U16)
         load_plane(nc.sync, wb_plane, wb_scales)
@@ -97,42 +97,42 @@ def tile_list_postedcodes_kernel(tc, xt_words, xt_scales, xo_words, xo_scales, w
         for t in range(PACK):
             nc.vector.tensor_copy(picked[t][:], stores[t][:].indirect(l3[:]))
         nc.scalar.activation(bars[0][:], picked[0][:].bitcast(FP8), ACT.Copy)
-        nc.scalar.activation(boards[0][:].indirect(l4[:]), bars[0][:], ACT.Copy, scale=steps[:, 0:1])
-        for t in (1, 3, 2):
-            nc.vector.tensor_scalar(bars[t][:], picked[t][:].bitcast(FP8), steps[:, t : t + 1], None, ALU.mult)
-        for t in (1, 2):
-            nc.scalar.activation(boards[t][:].indirect(l4[:]), bars[t][:], ACT.Copy)
-        nc.vector.tensor_copy(boards[3][:].indirect(l4[:]), bars[3][:])
-
         w_d = deal(nc.scalar.copy, "w_d", w_sb, U32)
+        nc.scalar.activation(bars[1][:], picked[1][:].bitcast(FP8), ACT.Copy, scale=steps[:, 1:2])
+        nc.vector.tensor_copy(boards[1][:].indirect(l4[:]), bars[1][:])
+        for t in (2, 3):
+            nc.gpsimd.tensor_copy(bars[t][:], picked[t][:].bitcast(FP8))
+        for t in (0, 2, 3):
+            nc.scalar.activation(boards[t][:].indirect(l4[:]), bars[t][:], ACT.Copy, scale=steps[:, t : t + 1])
+
         xt_g = tile("xt_g", J, U16)
         xt_gs = tile("xt_gs", J, U8)
         xo_g = tile("xo_g", J, U32)
         xo_gs = tile("xo_gs", J, U8)
         nc.vector.tensor_copy(xt_g[:], xt_sb[:].indirect(l1[:]))
         nc.vector.tensor_copy(xt_gs[:], xt_plane[:].indirect(l1[:]))
-        w_ds = deal(nc.vector.tensor_copy, "w_ds", w_plane, U8)
+        w0_ds = deal(nc.gpsimd.tensor_copy, "w0_ds", w0_plane, U8, "picked3")
+        w_ds = deal(nc.gpsimd.tensor_copy, "w_ds", w_plane, U8, "w0_plane")
+        w0_d = deal(nc.vector.tensor_copy, "w0_d", w0_sb, U16)
         nc.vector.tensor_copy(xo_g[:], xo_sb[:].indirect(l2[:]))
         nc.vector.tensor_copy(xo_gs[:], xo_plane[:].indirect(l2[:]))
-        w0_d = deal(nc.scalar.copy, "w0_d", w0_sb, U16)
-        w0_ds = deal(nc.vector.tensor_copy, "w0_ds", w0_plane, U8)
 
-        for t in range(PACK - 1):
+        nc.vector.tensor_copy(taken[1][:], boards[1][:].indirect(l5[:]))
+        for t in (0, 2, 3):
             nc.scalar.activation(taken[t][:], boards[t][:].indirect(l5[:]), ACT.Copy)
-        nc.vector.tensor_copy(taken[PACK - 1][:], boards[PACK - 1][:].indirect(l5[:]))
 
         accs = [ps.tile([P, J], F32, name="acc%d" % t) for t in range(PACK)]
-        for t in range(PACK):
+        for t in (1, 0, 2, 3):
             cols = slice(t * P, (t + 1) * P)
             nc.tensor.matmul_mx(accs[t][:], lhsT=w_d[:, cols].bitcast(FP8X4), lhsT_scale=w_ds[:, cols],
                                 rhs=xt_g[:].bitcast(FP4X4), rhs_scale=xt_gs[:], start=True, stop=False)
         diff = sb.tile([P, PACK, J], F32, name="diff")
-        for t in range(PACK):
+        for t in (1, 0, 2, 3):
             cols = slice(t * P, (t + 1) * P)
             nc.tensor.matmul_mx(accs[t][:], lhsT=w0_d[:, cols].bitcast(FP4X4), lhsT_scale=w0_ds[:, cols],
                                 rhs=xo_g[:].bitcast(FP8X4), rhs_scale=xo_gs[:], start=False, stop=True)
         halves = [slice(h * P, (h + 1) * P) for h in range(J // P)]
-        for t in range(PACK - 1):
+        for t in (1, 0, 2):
             nc.vector.tensor_tensor(diff[:, t, :], accs[t][:], taken[t][:], ALU.subtract)
         t = PACK - 1
         for half in halves:

from contextlib import ExitStack

import concourse.mybir as mybir

K, T, J, R, F, Z, C, V, I, N = 512, 1024, 256, 512, 512, 1024, 512, 1024, 256, 256
FLOPS = 2 * J * (K * R + F * R + R * N)

F32 = mybir.dt.float32
BF16 = mybir.dt.bfloat16
I32 = mybir.dt.int32
U32 = mybir.dt.uint32
U16 = mybir.dt.uint16
U8 = mybir.dt.uint8
FP8 = mybir.dt.float8_e4m3fn
FP8X4 = mybir.dt.float8_e4m3fn_x4
FP4X4 = mybir.dt.float4_e2m1fn_x4
ALU = mybir.AluOpType
ACT = mybir.ActivationFunctionType

P = 128
PACK = 4
QUADS = 4


def tile_list_postedcodes_kernel(tc, xt_words, xt_scales, xo_words, xo_scales, w_words, w_scales, w0_words, w0_scales,
                                      ca, st, wb_words, wb_scales, offs, offs2, offs3, offs4, offs5, out):
    nc = tc.nc
    with ExitStack() as ctx:
        lists = ctx.enter_context(tc.tile_pool(name="lists", bufs=1))
        sb = ctx.enter_context(tc.tile_pool(name="sb", bufs=1))
        ps = ctx.enter_context(tc.psum_pool(name="ps", bufs=1))

        def tile(name, cols, dtype, tag=None):
            return sb.tile([P, cols], dtype, name=name, tag=tag or name, align_bytes=64)

        def load_list(name, src):
            held = lists.tile([P, src.shape[1]], U16, name=name)
            nc.sync.dma_start(held[:], src)
            return held

        def load_words(queue, name, src, cols, dtype):
            held = tile(name, cols, dtype)
            queue.dma_start(held[:].bitcast(I32), src.bitcast(I32))
            return held

        def zeroed_plane(name, cols, engine=nc.vector):
            plane = tile(name, cols, U8)
            engine.memset(plane[:].bitcast(I32), 0)
            return plane

        def load_plane(queue, plane, src):
            for q in range(QUADS):
                queue.dma_start(plane[32 * q : 32 * q + 4, :].bitcast(I32), src[0, 4 * q : 4 * q + 4, :].bitcast(I32))

        def deal(engine_copy, name, src, dtype, tag=None):
            dealt = tile(name, R, dtype, tag)
            walk = "p m t" if dtype == U32 else "p t m"
            engine_copy(dealt[:].rearrange("p (t m) -> " + walk, t=PACK), src[:].rearrange("p (m t) -> " + walk, t=PACK))
            return dealt

        w0_plane = zeroed_plane("w0_plane", R, nc.gpsimd)
        xt_plane = zeroed_plane("xt_plane", T)
        w_plane = zeroed_plane("w_plane", R)
        boards = [tile("board%d" % t, C, F32) for t in range(PACK)]
        for t in range(PACK):
            nc.vector.memset(boards[t][:], 0.0)
        xo_plane = zeroed_plane("xo_plane", Z)
        wb_plane = zeroed_plane("wb_plane", N)

        ca_rows = ca.rearrange("(p t) v -> p t v", t=PACK)
        stores = [tile("store%d" % t, V, U8) for t in range(PACK)]
        l3 = load_list("l3", offs3)
        nc.sync.dma_start(stores[0][:], ca_rows[:, 0, :])
        nc.sync.dma_start(stores[1][:], ca_rows[:, 1, :])
        w_sb = load_words(nc.sync, "w_sb", w_words[0].rearrange("p n t -> p (n t)"), R, U32)
        l4 = load_list("l4", offs4)
        for t in range(2, PACK):
            nc.sync.dma_start(stores[t][:], ca_rows[:, t, :])
        steps = tile("steps", PACK, F32)
        nc.sync.dma_start(steps[:], st.rearrange("(p t) o -> p (t o)", t=PACK))
        load_plane(nc.gpsimd, w0_plane, w0_scales)
        l1 = load_list("l1", offs)
        xt_sb = load_words(nc.sync, "xt_sb", xt_words[0], T, U16)
        load_plane(nc.sync, xt_plane, xt_scales)
        load_plane(nc.sync, w_plane, w_scales)
        w0_sb = load_words(nc.sync, "w0_sb", w0_words[0], R, U16)
        l2 = load_list("l2", offs2)
        xo_sb = load_words(nc.sync, "xo_sb", xo_words[0].rearrange("p n t -> p (n t)"), Z, U32)
        load_plane(nc.sync, xo_plane, xo_scales)
        l5 = load_list("l5", offs5)
        wb_sb = load_words(nc.sync, "wb_sb", wb_words[0], N, U16)
        load_plane(nc.sync, wb_plane, wb_scales)

        picked = [tile("picked%d" % t, I, U8) for t in range(PACK)]
        bars = [tile("bars%d" % t, I, F32) for t in range(PACK)]
        taken = [tile("taken%d" % t, J, F32) for t in range(PACK)]
        for t in range(PACK):
            nc.vector.tensor_copy(picked[t][:], stores[t][:].indirect(l3[:]))
        nc.scalar.activation(bars[0][:], picked[0][:].bitcast(FP8), ACT.Copy)
        w_d = deal(nc.scalar.copy, "w_d", w_sb, U32)
        nc.scalar.activation(bars[1][:], picked[1][:].bitcast(FP8), ACT.Copy, scale=steps[:, 1:2])
        nc.vector.tensor_copy(boards[1][:].indirect(l4[:]), bars[1][:])
        for t in (2, 3):
            nc.gpsimd.tensor_copy(bars[t][:], picked[t][:].bitcast(FP8))
        for t in (0, 2, 3):
            nc.scalar.activation(boards[t][:].indirect(l4[:]), bars[t][:], ACT.Copy, scale=steps[:, t : t + 1])

        xt_g = tile("xt_g", J, U16)
        xt_gs = tile("xt_gs", J, U8)
        xo_g = tile("xo_g", J, U32)
        xo_gs = tile("xo_gs", J, U8)
        nc.vector.tensor_copy(xt_g[:], xt_sb[:].indirect(l1[:]))
        nc.vector.tensor_copy(xt_gs[:], xt_plane[:].indirect(l1[:]))
        w0_ds = deal(nc.gpsimd.tensor_copy, "w0_ds", w0_plane, U8, "picked3")
        w_ds = deal(nc.gpsimd.tensor_copy, "w_ds", w_plane, U8, "w0_plane")
        w0_d = deal(nc.vector.tensor_copy, "w0_d", w0_sb, U16)
        nc.vector.tensor_copy(xo_g[:], xo_sb[:].indirect(l2[:]))
        nc.vector.tensor_copy(xo_gs[:], xo_plane[:].indirect(l2[:]))

        nc.vector.tensor_copy(taken[1][:], boards[1][:].indirect(l5[:]))
        for t in (0, 2, 3):
            nc.scalar.activation(taken[t][:], boards[t][:].indirect(l5[:]), ACT.Copy)

        accs = [ps.tile([P, J], F32, name="acc%d" % t) for t in range(PACK)]
        for t in (1, 0, 2, 3):
            cols = slice(t * P, (t + 1) * P)
            nc.tensor.matmul_mx(accs[t][:], lhsT=w_d[:, cols].bitcast(FP8X4), lhsT_scale=w_ds[:, cols],
                                rhs=xt_g[:].bitcast(FP4X4), rhs_scale=xt_gs[:], start=True, stop=False)
        diff = sb.tile([P, PACK, J], F32, name="diff")
        for t in (1, 0, 2, 3):
            cols = slice(t * P, (t + 1) * P)
            nc.tensor.matmul_mx(accs[t][:], lhsT=w0_d[:, cols].bitcast(FP4X4), lhsT_scale=w0_ds[:, cols],
                                rhs=xo_g[:].bitcast(FP8X4), rhs_scale=xo_gs[:], start=False, stop=True)
        halves = [slice(h * P, (h + 1) * P) for h in range(J // P)]
        for t in (1, 0, 2):
            nc.vector.tensor_tensor(diff[:, t, :], accs[t][:], taken[t][:], ALU.subtract)
        t = PACK - 1
        for half in halves:
            nc.vector.tensor_tensor(diff[:, t, half], accs[t][:, half], taken[t][:, half], ALU.subtract)

        hids = [sb.tile([P, P, PACK], BF16, name="hid%d" % h, align_bytes=64) for h in range(2)]
        hid_codes = [tile("hid_codes%d" % h, P, U32) for h in range(2)]
        hid_scales = [tile("hid_scales%d" % h, P, U8) for h in range(2)]
        for h, half in enumerate(halves):
            nc.vector.tensor_scalar(hids[h][:].rearrange("p (c i) t -> p c t i", i=4),
                                    diff[:, :, half].rearrange("p t (c i) -> p c t i", i=4), 0.0, None, ALU.max)
        for h in range(2):
            nc.vector.quantize_mx(hid_codes[h][:].bitcast(FP8X4), hid_scales[h][:], hids[h][:].rearrange("p j t -> p (j t)"))

        for h, half in enumerate(halves):
            for u, (copy, queue) in enumerate(((nc.scalar.copy, nc.scalar), (nc.vector.tensor_copy, nc.sync))):
                cols = slice(u * P, (u + 1) * P)
                res = ps.tile([P, P], F32, name="res%d%d" % (h, u))
                nc.tensor.matmul_mx(res[:], lhsT=wb_sb[:, cols].bitcast(FP4X4), lhsT_scale=wb_plane[:, cols],
                                    rhs=hid_codes[h][:].bitcast(FP8X4), rhs_scale=hid_scales[h][:], start=True, stop=True)
                done = tile("done%d%d" % (h, u), P, F32)
                copy(done[:], res[:])
                queue.dma_start(out[cols, half], done[:])
